import numpy as np
import ml_dtypes


def mxq(x, axis, fmt="e4m3"):
    dtype, down = {"e4m3": (ml_dtypes.float8_e4m3fn, 7), "e5m2": (ml_dtypes.float8_e5m2, 14)}[fmt]
    v = np.moveaxis(np.asarray(x, np.float32).astype(ml_dtypes.bfloat16).astype(np.float64), axis, -1)
    blocks = v.reshape(v.shape[:-1] + (-1, 32))
    amax = np.abs(blocks).max(-1, keepdims=True)
    byte = np.maximum(np.where(amax > 0, np.frexp(amax)[1] - 1 + 127, 0) - down, 1)
    scale = np.exp2(byte - 127.0)
    codes = (blocks / scale).astype(np.float32).astype(dtype).astype(np.float64)
    return np.moveaxis((codes * scale).reshape(v.shape), -1, axis)


WIDE = False


def mx_kscale(k):
    if not WIDE:
        return np.ones(k)
    levels = np.array([10, -10, 5, -5, 0])
    if k % 512:
        return np.exp2(np.random.permutation(np.resize(levels, k // 32))).repeat(32)
    a = np.empty((k // 512, 16))
    for p in range(k // 512):
        a[p, :8] = np.random.permutation(np.resize(levels, 8))
        for g in range(8):
            far = levels[np.abs(levels - a[p, g]) >= 10]
            a[p, g + 8] = far[np.random.randint(len(far))]
    return np.exp2(a.ravel()).repeat(32)


def f64(x):
    return np.asarray(x).astype(np.float64)


def striped(idx):
    return np.tile(idx.reshape(-1, 16).T, (8, 1)).astype(np.uint16)


def unstriped(offs):
    return offs[:16].T.reshape(-1).astype(np.int64)


def pack_weight(w):
    k, n = w.shape
    w = f64(np.asarray(w, np.float32).astype(ml_dtypes.bfloat16)).reshape(k // 32, 32, n)
    amax = np.abs(w).max(1)
    byte = np.clip(np.where(amax > 0, np.frexp(amax)[1] - 1 + 127 - 7, 1), 1, 254)
    scaled = (w * np.exp2(127.0 - byte)[:, None, :]).reshape(k, n).astype(np.float32)
    words = np.ascontiguousarray(scaled.reshape(k // 512, 128, 4, n).transpose(0, 1, 3, 2)).astype(ml_dtypes.float8_e4m3fn).view(np.uint8)
    return words, np.ascontiguousarray(byte.astype(np.uint8).reshape(k // 512, 16, n))


def unpack_weight(words, scales):
    g, p, n, _ = words.shape
    vals = np.ascontiguousarray(words).view(ml_dtypes.float8_e4m3fn).astype(np.float64) * np.repeat(np.exp2(scales.astype(np.float64) - 127.0), 8, axis=1)[..., None]
    return vals.transpose(0, 1, 3, 2).reshape(g * 512, n)


def relu(v):
    return np.maximum(v, 0.0)

def planes(y):
    n, m = y.shape
    v = y.astype(np.float32).astype(ml_dtypes.bfloat16).astype(np.float64).reshape(n // 32, 32, m)
    top = np.abs(v).max(1)
    byte = np.clip(np.where(top > 0, np.frexp(top)[1] - 1 + 127 - 7, 1), 1, 254)
    codes = (v * np.exp2(127.0 - byte)[:, None, :]).reshape(n, m).astype(np.float32).astype(ml_dtypes.float8_e4m3fn).view(np.uint8)
    words = codes.reshape(n // 512, 128, 4, m).transpose(0, 1, 3, 2)
    return np.ascontiguousarray(words), np.ascontiguousarray(byte.astype(np.uint8).reshape(n // 512, 16, m))


K, T, S, H, U = 512, 1024, 512, 512, 1024
P = 2 ** 7


def setup_inputs():
    n = np.random.standard_normal
    s = mx_kscale(K)[:, None]
    u = mx_kscale(H)
    packed_xT = pack_weight(n((K, T)) * s)
    return {
        "x_words": packed_xT[0],
        "x_scales": packed_xT[1],
        "gate": np.tile(np.random.uniform(0.5, 1.5, S), (P, 1)).astype(np.float32),
        "w1": (n((K, H)) / np.sqrt(K) / s * u).astype(np.float32),
        "w2": (n((H, H)) / np.sqrt(H) / u[:, None]).astype(np.float32),
        "offs": striped(np.random.permutation(T)[:S]),
        "dst": striped(np.random.permutation(U)[:S]),
    }


def reference(x_words, x_scales, gate, w1, w2, offs, dst):
    xq = unpack_weight(x_words, x_scales)[:, unstriped(offs)]
    h = relu(mxq(f64(w1), 0, "e4m3").T @ xq)
    y = mxq(f64(w2), 0, "e4m3").T @ mxq(h, 0, "e4m3")
    out = np.zeros((H, U))
    out[:, unstriped(dst)] = y * f64(gate)[:1]
    return (out,) + planes(out)

from contextlib import ExitStack

import concourse.mybir as mybir

F32 = mybir.dt.float32
BF16 = mybir.dt.bfloat16
I32 = mybir.dt.int32
U32 = mybir.dt.uint32
U16 = mybir.dt.uint16
U8 = mybir.dt.uint8
FP8X4 = mybir.dt.float8_e4m3fn_x4
MULT = mybir.AluOpType.mult
RELU = mybir.ActivationFunctionType.Relu
COPY = mybir.ActivationFunctionType.Copy

P = 128
PACK = 4
K, T, S, H, U = 512, 1024, 512, 512, 1024
LIST_ROWS = 16
CHUNK = 128
HALF = 256
VECTOR_SHARE = 224
SCALAR_COLUMNS = 416
QUARTER = 256

FLOPS = 2 * K * H * S + 2 * H * H * S


def tile_picked_route2_mlprelu_po_kernel(
    tc, x_words, x_scales, gate, w1, w2, offs, dst, out_0, out_1, out_2
):
    nc = tc.nc
    with ExitStack() as ctx:
        keep = ctx.enter_context(tc.tile_pool(name="keep", bufs=1))
        psum = ctx.enter_context(tc.psum_pool(name="psum", bufs=1))

        offs_t = keep.tile([P, S // LIST_ROWS], U16, name="offs_t")
        dst_t = keep.tile([P, S // LIST_ROWS], U16, name="dst_t")
        xw = keep.tile([P, T], U32, name="xw", align_bytes=64)
        xs = keep.tile([P, T], U8, name="xs", align_bytes=64)
        pieces = [(0, CHUNK), (CHUNK, CHUNK), (HALF, HALF)]
        gate_t = [keep.tile([P, n], F32, name="gate%d" % lo, tag="gate%d" % lo, align_bytes=64) for lo, n in pieces]
        raw = {}
        for name in ("w1", "w2"):
            for h in range(2):
                raw[name, h] = keep.tile([P, PACK, H // 2], F32, name="raw_%s_%d" % (name, h), tag="raw_%s_%d" % (name, h), align_bytes=64)

        for q in range(4):
            nc.sync.dma_start(
                out=xs[32 * q : 32 * (q + 1), :].bitcast(I32),
                in_=x_scales[0, 4 * q : 4 * q + 4, :].bitcast(I32).partition_broadcast(8),
            )

        def load_weight(name, w):
            rows = w.rearrange("(p j) c -> p j c", j=PACK)
            for h in range(2):
                nc.sync.dma_start(out=raw[name, h][:], in_=rows[:, :, h * (H // 2) : (h + 1) * (H // 2)])

        nc.sync.dma_start(out=offs_t[:], in_=offs)
        nc.sync.dma_start(out=xw[:].bitcast(I32), in_=x_words[0].rearrange("p n t -> p (n t)").bitcast(I32))
        load_weight("w1", w1)
        load_weight("w2", w2)
        nc.sync.dma_start(out=dst_t[:], in_=dst)
        for k, (lo, n) in enumerate(pieces):
            nc.sync.dma_start(out=gate_t[k][:], in_=gate[:, lo : lo + n])

        windows = [keep.tile([P, U], F32, name="window%d" % t, align_bytes=64) for t in range(PACK)]
        for t in (2, 3, 1, 0):
            nc.gpsimd.memset(windows[t][:], 0.0)

        gs = keep.tile([P, S], U8, name="gs", align_bytes=64)
        gw = keep.tile([P, S], U32, name="gw", align_bytes=64)
        nc.vector.tensor_copy(out=gs[:], in_=xs[:].indirect(offs_t[:]))

        grouped, codes, scales = {}, {}, {}
        for name in ("w1", "w2"):
            grouped[name] = keep.tile([P, PACK * H], BF16, name="grouped_" + name, tag="grouped_" + name, align_bytes=64)
            codes[name] = keep.tile([P, H], U32, name="codes_" + name, align_bytes=64)
            scales[name] = keep.tile([P, H], U8, name="scales_" + name, align_bytes=64)

        def deal(copy, name, h, lo, hi):
            dealt = grouped[name][:].rearrange("p (t m j) -> p m t j", t=PACK, j=PACK)[:, 64 * h + lo : 64 * h + hi]
            copy(out=dealt, in_=raw[name, h][:].rearrange("p j (m t) -> p m t j", t=PACK)[:, lo:hi])

        def quantize_weight(name, lo, hi):
            nc.vector.quantize_mx(
                out=codes[name][:, lo:hi].bitcast(FP8X4), scales=scales[name][:, lo:hi], in_=grouped[name][:, PACK * lo : PACK * hi]
            )

        nc.vector.tensor_copy(out=gw[:], in_=xw[:].indirect(offs_t[:]))
        deal(nc.vector.tensor_copy, "w1", 0, 0, 64)
        deal(nc.scalar.copy, "w1", 1, 0, 24)
        deal(nc.vector.tensor_copy, "w1", 1, 24, 64)
        quantize_weight("w1", 0, 2 * P)
        quantize_weight("w1", 2 * P, 4 * P)
        deal(nc.scalar.copy, "w2", 0, 0, 64)
        deal(nc.vector.tensor_copy, "w2", 1, 0, 64)

        h_grouped = [
            keep.tile([P, PACK * n], BF16, name="h_grouped%d" % lo, tag=tag, align_bytes=64)
            for (lo, n), tag in zip(pieces, ("raw_w2_0", "h_grouped1", "h_grouped2"))
        ]
        h_codes = {}
        h_scales = [keep.tile([P, n], U8, name="h_scales%d" % lo, align_bytes=64) for lo, n in pieces]
        for k, (lo, n) in enumerate(pieces):
            for c in range(0, n, CHUNK):
                bank = psum.tile([P, PACK, CHUNK], F32, name="first%d" % (lo + c), tag="bank%d" % ((lo + c) // CHUNK))
                for t in range(PACK):
                    nc.tensor.matmul_mx(
                        out=bank[:, t, :],
                        lhsT=codes["w1"][:, t * P : (t + 1) * P].bitcast(FP8X4),
                        lhsT_scale=scales["w1"][:, t * P : (t + 1) * P],
                        rhs=gw[:, lo + c : lo + c + CHUNK].bitcast(FP8X4),
                        rhs_scale=gs[:, lo + c : lo + c + CHUNK],
                        start=True,
                        stop=True,
                    )
                nc.scalar.activation(
                    out=h_grouped[k][:, PACK * c : PACK * (c + CHUNK)].rearrange("p (n t) -> p n t", t=PACK),
                    in_=bank[:].rearrange("p t n -> p n t"),
                    func=RELU,
                )

        gated = [keep.tile([P, 2, S], F32, name="gated%d" % pair, align_bytes=64) for pair in range(2)]

        def quantize_hidden(k, tag):
            h_codes[k] = keep.tile([P, pieces[k][1]], U32, name="h_codes%d" % k, tag=tag, align_bytes=64)
            nc.vector.quantize_mx(out=h_codes[k][:].bitcast(FP8X4), scales=h_scales[k][:], in_=h_grouped[k][:])

        def second_product(pair, k, tag):
            lo, n = pieces[k]
            bank = psum.tile([P, 2, n], F32, name="second%d_%d" % (pair, lo), tag=tag)
            for e in range(2):
                t = 2 * pair + e
                nc.tensor.matmul_mx(
                    out=bank[:, e, :],
                    lhsT=codes["w2"][:, t * P : (t + 1) * P].bitcast(FP8X4),
                    lhsT_scale=scales["w2"][:, t * P : (t + 1) * P],
                    rhs=h_codes[k][:].bitcast(FP8X4),
                    rhs_scale=h_scales[k][:],
                    start=True,
                    stop=True,
                )
            nc.vector.tensor_tensor(
                out=gated[pair][:, :, lo : lo + n],
                in0=bank[:],
                in1=gate_t[k][:].unsqueeze(1).to_broadcast([P, 2, n]),
                op=MULT,
            )

        quantize_hidden(0, "raw_w2_1")
        quantize_weight("w2", 2 * P, 4 * P)
        quantize_weight("w2", 0, 2 * P)
        quantize_hidden(1, "grouped_w2")
        second_product(1, 0, "bank4")
        second_product(0, 0, "bank5")
        quantize_hidden(2, "gate0")
        second_product(1, 1, "bank6")
        second_product(0, 1, "bank7")
        second_product(1, 2, "bank0")
        second_product(0, 2, "bank1")

        def target(t, lo, hi):
            return windows[t][:].indirect(dst_t[:, lo // LIST_ROWS : hi // LIST_ROWS])

        def scatter_on_scalar(t, lo, hi):
            nc.scalar.activation(out=target(t, lo, hi), in_=gated[t // 2][:, t % 2, lo:hi], func=COPY)

        def scatter_on_vector(t, lo, hi):
            nc.vector.tensor_copy(out=target(t, lo, hi), in_=gated[t // 2][:, t % 2, lo:hi])

        out_rows = out_0.rearrange("(p t) u -> p t u", t=PACK)
        rounded = keep.tile([P, PACK, U], BF16, name="rounded", align_bytes=64)

        def store(t):
            nc.sync.dma_start(out=out_rows[:, t, :], in_=windows[t][:])

        def round_rows(copy, t, lo, hi):
            copy(out=rounded[:, t, lo:hi], in_=windows[t][:, lo:hi])

        scatter_on_scalar(2, 0, CHUNK)
        scatter_on_scalar(2, CHUNK, HALF)
        scatter_on_scalar(0, 0, HALF)
        scatter_on_scalar(2, HALF, S)
        store(2)
        scatter_on_scalar(0, HALF, S)
        scatter_on_vector(1, 0, HALF)
        scatter_on_vector(3, S - VECTOR_SHARE, S)
        scatter_on_vector(1, HALF, S)
        store(0)
        store(1)
        round_rows(nc.vector.tensor_copy, 2, 0, U)
        round_rows(nc.vector.tensor_copy, 1, 0, U)
        round_rows(nc.vector.tensor_copy, 0, 0, U)
        scatter_on_scalar(3, 0, S - VECTOR_SHARE)
        store(3)
        round_rows(nc.scalar.copy, 3, 0, SCALAR_COLUMNS)
        round_rows(nc.vector.tensor_copy, 3, SCALAR_COLUMNS, U)

        y_codes = keep.tile([P, U], U32, name="y_codes", align_bytes=64)
        y_scales = keep.tile([P, U], U8, name="y_scales", align_bytes=64)
        y_grouped = keep.tile([P, U, PACK], BF16, name="y_grouped", align_bytes=64)
        out_words = out_1[0].rearrange("p n t -> p (n t)").bitcast(I32)

        def weave(copy, lo, hi):
            copy(out=y_grouped[:, lo:hi, :], in_=rounded[:, :, lo:hi].rearrange("p t u -> p u t"))

        def quantize_out(q):
            cols = slice(q * QUARTER, (q + 1) * QUARTER)
            nc.vector.quantize_mx(
                out=y_codes[:, cols].bitcast(FP8X4), scales=y_scales[:, cols], in_=y_grouped[:, cols, :].rearrange("p u t -> p (u t)")
            )
            nc.sync.dma_start(out=out_words[:, cols], in_=y_codes[:, cols].bitcast(I32))

        weave(nc.scalar.copy, 0, QUARTER)
        weave(nc.scalar.copy, QUARTER, SCALAR_COLUMNS)
        weave(nc.vector.tensor_copy, 3 * QUARTER, U)
        weave(nc.vector.tensor_copy, SCALAR_COLUMNS, 3 * QUARTER)
        for q in (3, 0, 2, 1):
            quantize_out(q)
        for q in range(4):
            engine = nc.sync if q % 2 == 0 else nc.scalar
            engine.dma_start(out=out_2[0, 4 * q : 4 * q + 4, :].bitcast(I32), in_=y_scales[32 * q : 32 * q + 4, :].bitcast(I32))
